import numpy as np
import ml_dtypes


def mxq(x, axis, fmt="e4m3"):
    dtype, down = {"e4m3": (ml_dtypes.float8_e4m3fn, 7), "e5m2": (ml_dtypes.float8_e5m2, 14)}[fmt]
    v = np.moveaxis(np.asarray(x, np.float32).astype(ml_dtypes.bfloat16).astype(np.float64), axis, -1)
    blocks = v.reshape(v.shape[:-1] + (-1, 32))
    amax = np.abs(blocks).max(-1, keepdims=True)
    byte = np.maximum(np.where(amax > 0, np.frexp(amax)[1] - 1 + 127, 0) - down, 1)
    scale = np.exp2(byte - 127.0)
    codes = (blocks / scale).astype(np.float32).astype(dtype).astype(np.float64)
    return np.moveaxis((codes * scale).reshape(v.shape), -1, axis)


WIDE = False


def mx_kscale(k):
    if not WIDE:
        return np.ones(k)
    levels = np.array([10, -10, 5, -5, 0])
    if k % 512:
        return np.exp2(np.random.permutation(np.resize(levels, k // 32))).repeat(32)
    a = np.empty((k // 512, 16))
    for p in range(k // 512):
        a[p, :8] = np.random.permutation(np.resize(levels, 8))
        for g in range(8):
            far = levels[np.abs(levels - a[p, g]) >= 10]
            a[p, g + 8] = far[np.random.randint(len(far))]
    return np.exp2(a.ravel()).repeat(32)


def f64(x):
    return np.asarray(x).astype(np.float64)


def striped(idx):
    return np.tile(idx.reshape(-1, 16).T, (8, 1)).astype(np.uint16)


def unstriped(offs):
    return offs[:16].T.reshape(-1).astype(np.int64)


def striped8(idx):
    return np.concatenate([x.reshape(-1, 16).T for x in idx]).astype(np.uint16)


def runs(offs, k):
    lists = np.stack([offs[16 * r : 16 * r + 16].T.reshape(-1) for r in range(8)]).astype(np.int64)
    return lists[np.arange(k) % 512 // 64]


def pack_weight(w):
    k, n = w.shape
    w = f64(np.asarray(w, np.float32).astype(ml_dtypes.bfloat16)).reshape(k // 32, 32, n)
    amax = np.abs(w).max(1)
    byte = np.clip(np.where(amax > 0, np.frexp(amax)[1] - 1 + 127 - 7, 1), 1, 254)
    scaled = (w * np.exp2(127.0 - byte)[:, None, :]).reshape(k, n).astype(np.float32)
    words = np.ascontiguousarray(scaled.reshape(k // 512, 128, 4, n).transpose(0, 1, 3, 2)).astype(ml_dtypes.float8_e4m3fn).view(np.uint8)
    return words, np.ascontiguousarray(byte.astype(np.uint8).reshape(k // 512, 16, n))


def unpack_weight(words, scales):
    g, p, n, _ = words.shape
    vals = np.ascontiguousarray(words).view(ml_dtypes.float8_e4m3fn).astype(np.float64) * np.repeat(np.exp2(scales.astype(np.float64) - 127.0), 8, axis=1)[..., None]
    return vals.transpose(0, 1, 3, 2).reshape(g * 512, n)

def planes(y):
    n, m = y.shape
    v = y.astype(np.float32).astype(ml_dtypes.bfloat16).astype(np.float64).reshape(n // 32, 32, m)
    top = np.abs(v).max(1)
    byte = np.clip(np.where(top > 0, np.frexp(top)[1] - 1 + 127 - 7, 1), 1, 254)
    codes = (v * np.exp2(127.0 - byte)[:, None, :]).reshape(n, m).astype(np.float32).astype(ml_dtypes.float8_e4m3fn).view(np.uint8)
    words = codes.reshape(n // 512, 128, 4, m).transpose(0, 1, 3, 2)
    return np.ascontiguousarray(words), np.ascontiguousarray(byte.astype(np.uint8).reshape(n // 512, 16, m))


K, T, S, G, H, C, W = 512, 1024, 256, 2048, 512, 512, 192


def setup_inputs():
    n = np.random.standard_normal
    s = mx_kscale(K)[:, None]
    packed_xT = pack_weight(n((K, T)) * s)
    packed_dT = pack_weight(n((K, G)) / s)
    return {
        "x_words": packed_xT[0],
        "x_scales": packed_xT[1],
        "d_words": packed_dT[0],
        "d_scales": packed_dT[1],
        "gs": (np.random.uniform(0.5, 1.5, (K, 1)) / s).astype(np.float32),
        "offs": striped(np.random.permutation(T)[:S]),
        "k1": striped8(np.random.randint(0, G, (8, H))),
        "n1": striped8(np.stack([np.random.permutation(S) for _ in range(8)])),
        "n2": striped8(np.stack([np.random.permutation(S) for _ in range(8)])),
        "n3": striped8(np.stack([np.random.permutation(S) for _ in range(8)])),
        "cand": striped8(np.random.randint(0, T, (8, C))),
        "n4": striped(np.random.permutation(S)[:W]),
        "n5": striped(np.random.permutation(S)[:W]),
    }


def reference(x_words, x_scales, d_words, d_scales, gs, offs, k1, n1, n2, n3, cand, n4, n5):
    x_cand = unpack_weight(x_words, x_scales)[np.arange(K)[:, None], runs(cand, K)]
    d_k1 = unpack_weight(d_words, d_scales)[np.arange(K)[:, None], runs(k1, K)]
    xq = unpack_weight(x_words, x_scales)[:, unstriped(offs)]
    h = 0.0625 * (d_k1.T @ xq)
    st = h[np.arange(H)[:, None], runs(n1, H)] - (h[np.arange(H)[:, None], runs(n2, H)])
    z = f64(gs) * (np.maximum(st, st[np.arange(H)[:, None], runs(n3, H)]))
    s = 0.0625 * ((x_cand.T @ mxq(z, 0, "e4m3")))
    old = s[:, unstriped(n4)]
    pa = s[:, unstriped(n5)]
    ra = old - (0.5 * pa)
    out = s.copy()
    out[:, unstriped(n4)] = ra
    return (out,) + planes(out)

@@ -1,0 +1,206 @@
+from contextlib import ExitStack
+
+import concourse.mybir as mybir
+
+K, T, S, G, H, C, W = 512, 1024, 256, 2048, 512, 512, 192
+FLOPS = 2 * K * H * S + 2 * K * C * S
+
+F32 = mybir.dt.float32
+BF16 = mybir.dt.bfloat16
+I32 = mybir.dt.int32
+U32 = mybir.dt.uint32
+U16 = mybir.dt.uint16
+U8 = mybir.dt.uint8
+FP8X4 = mybir.dt.float8_e4m3fn_x4
+ALU = mybir.AluOpType
+COPY = mybir.ActivationFunctionType.Copy
+
+P = 128
+PACK = 4
+HALF = S // 2
+WIN = 2 * S
+
+
+def tile_picked_pqhcgapmxkdif_none_po_kernel(
+    tc, x_words, x_scales, d_words, d_scales, gs, offs, k1, n1, n2, n3, cand, n4, n5, out_0, out_1, out_2
+):
+    nc = tc.nc
+    with ExitStack() as ctx:
+        lists = ctx.enter_context(tc.tile_pool(name="lists", bufs=1))
+        sb = ctx.enter_context(tc.tile_pool(name="sb", bufs=1))
+        ps = ctx.enter_context(tc.psum_pool(name="ps", bufs=1))
+
+        def load_list(name, src):
+            tile = lists.tile(list(src.shape), U16, name=name)
+            nc.sync.dma_start(tile[:], src)
+            return tile
+
+        def zeroed_bytes(name, width, tag=""):
+            tile = sb.tile([P, width], U8, name=name, align_bytes=64)
+            nc.vector.memset(tile[:].bitcast(I32), 0)
+            return tile
+
+        def load_scale_rows(tile, src):
+            nc.sync.dma_start(tile[0:P:8, :].bitcast(I32), src[0].bitcast(I32))
+
+        def load_words(name, src, width):
+            tile = sb.tile([P, width], U32, name=name, align_bytes=64)
+            nc.scalar.dma_start(tile[:].bitcast(I32), src[0].rearrange("p c r -> p (c r)").bitcast(I32))
+            return tile
+
+        def place_scale_rows(queue, dst, src):
+            for r in range(4):
+                queue.dma_start(dst[r:P:32, :].bitcast(I32), src[8 * r : P : 32, :].bitcast(I32))
+
+        def deal(dst, src, t0, t1):
+            nc.vector.tensor_copy(dst[:, t0:t1, :], src.rearrange("p (m t) -> p t m", t=PACK)[:, t0:t1, :])
+
+        d_scale_tab = zeroed_bytes("d_scale_tab", G)
+        x_scale_tab = sb.tile([P, T], U8, name="x_scale_tab", align_bytes=64)
+        nc.gpsimd.memset(x_scale_tab[:].bitcast(I32), 0)
+        k1_l = load_list("k1_l", k1)
+        load_scale_rows(d_scale_tab, d_scales)
+        offs_l = load_list("offs_l", offs)
+        load_scale_rows(x_scale_tab, x_scales)
+        d_tab = load_words("d_tab", d_words, G)
+        x_tab = load_words("x_tab", x_words, T)
+        n1_l = load_list("n1_l", n1)
+        n2_l = load_list("n2_l", n2)
+        n3_l = load_list("n3_l", n3)
+        cand_l = load_list("cand_l", cand)
+        n4_l = load_list("n4_l", n4)
+        n5_l = load_list("n5_l", n5)
+        gain = sb.tile([P, PACK], F32, name="gain")
+        nc.gpsimd.dma_start(gain[:], gs.rearrange("(p t) o -> p (t o)", t=PACK))
+        placed1 = zeroed_bytes("placed1", H + S)
+        placed2 = zeroed_bytes("placed2", C)
+
+        picked1 = sb.tile([P, H + S], U8, name="picked1", align_bytes=64)
+        nc.vector.tensor_copy(picked1[:, :H], d_scale_tab[:].indirect(k1_l[:]))
+        nc.vector.tensor_copy(picked1[:, H:], x_scale_tab[:].indirect(offs_l[:]))
+        place_scale_rows(nc.scalar, placed1, picked1)
+        d_picked = sb.tile([P, H], U32, name="d_picked", align_bytes=64)
+        nc.vector.tensor_copy(d_picked[:], d_tab[:].indirect(k1_l[:]))
+        d_codes = sb.tile([P, PACK, P], U32, name="d_codes", align_bytes=64)
+        d_bytes = sb.tile([P, PACK, P], U8, name="d_bytes", align_bytes=64)
+        deal(d_codes, d_picked[:], 0, 1)
+        xq = sb.tile([P, S], U32, name="xq", tag="xq", align_bytes=64)
+        nc.vector.tensor_copy(xq[:], x_tab[:].indirect(offs_l[:]))
+        deal(d_bytes, placed1[:, :H], 0, 1)
+        deal(d_codes, d_picked[:], 1, PACK)
+        deal(d_bytes, placed1[:, :H], 1, PACK)
+
+        h = []
+        for t in range(PACK):
+            acc = ps.tile([P, S], F32, name=f"h_acc{t}", tag=f"bank{t}")
+            nc.tensor.matmul_mx(
+                out=acc[:], lhsT=d_codes[:, t, :].bitcast(FP8X4), lhsT_scale=d_bytes[:, t, :],
+                rhs=xq[:].bitcast(FP8X4), rhs_scale=placed1[:, H:], start=True, stop=True,
+            )
+            h_t = sb.tile([P, WIN], F32, name=f"h{t}", tag=f"h{t}", align_bytes=64)
+            if t == 0:
+                nc.scalar.activation(h_t[:, :S], acc[:], COPY, scale=0.0625)
+            else:
+                nc.vector.tensor_scalar(h_t[:, :S], acc[:], 0.0625, None, ALU.mult)
+            h.append(h_t)
+
+        z_bf = [sb.tile([P, HALF, PACK], BF16, name=f"z_bf{c}", align_bytes=64) for c in range(2)]
+        st = []
+
+        def differences(t):
+            a = sb.tile([P, S], F32, name=f"a{t}")
+            b = sb.tile([P, S], F32, name=f"b{t}")
+            nc.scalar.activation(a[:], h[t][:].indirect(n1_l[:]), COPY)
+            nc.scalar.activation(b[:], h[t][:].indirect(n2_l[:]), COPY)
+            st_t = sb.tile([P, WIN], F32, name=f"st{t}")
+            nc.vector.tensor_tensor(st_t[:, :S], a[:], b[:], ALU.subtract)
+            st.append(st_t)
+
+        def larger(t, c0, c1):
+            cols = slice(c0 * HALF, c1 * HALF)
+            width = (c1 - c0) * HALF
+            g = sb.tile([P, width], F32, name=f"g{t}_{c0}")
+            nc.scalar.activation(g[:], st[t][:].indirect(n3_l[:, c0 * HALF // 16 : c1 * HALF // 16]), COPY)
+            m = sb.tile([P, width], F32, name=f"m{t}_{c0}")
+            nc.vector.tensor_tensor(m[:], g[:], st[t][:, cols], ALU.max)
+            for c in range(c0, c1):
+                nc.vector.tensor_scalar(
+                    z_bf[c][:, :, t], m[:, (c - c0) * HALF : (c - c0 + 1) * HALF], gain[:, t : t + 1], None, ALU.mult
+                )
+
+        differences(0)
+        differences(1)
+        picked2 = sb.tile([P, C], U8, name="picked2", tag="xq", align_bytes=64)
+        nc.vector.tensor_copy(picked2[:], x_scale_tab[:].indirect(cand_l[:]))
+        place_scale_rows(nc.sync, placed2, picked2)
+        larger(0, 0, 2)
+        differences(2)
+        c_picked = sb.tile([P, C], U32, name="c_picked", tag="h0", align_bytes=64)
+        nc.vector.tensor_copy(c_picked[:], x_tab[:].indirect(cand_l[:]))
+        larger(1, 0, 2)
+        c_codes = sb.tile([P, PACK, P], U32, name="c_codes", align_bytes=64)
+        c_bytes = sb.tile([P, PACK, P], U8, name="c_bytes", align_bytes=64)
+        deal(c_codes, c_picked[:], 0, PACK)
+        deal(c_bytes, placed2[:], 0, PACK)
+        differences(3)
+        larger(2, 0, 2)
+
+        s = [sb.tile([P, S], F32, name=f"s{t}") for t in range(PACK)]
+        s_acc = [ps.tile([P, S], F32, name=f"s_acc{t}", tag=f"bank{t + 4 if t < 3 else 0}") for t in range(PACK)]
+        s0_last = ps.tile([P, HALF], F32, name="s0_last", tag="bank7")
+        for c in range(2):
+            larger(3, c, c + 1)
+            z_codes = sb.tile([P, HALF], U32, name=f"z_codes{c}", align_bytes=64)
+            z_bytes = sb.tile([P, HALF], U8, name=f"z_bytes{c}", align_bytes=64)
+            nc.vector.quantize_mx(
+                out=z_codes[:].bitcast(FP8X4), scales=z_bytes[:], in_=z_bf[c][:].rearrange("p j t -> p (j t)")
+            )
+            cols = slice(c * HALF, (c + 1) * HALF)
+            for t in range(PACK):
+                acc = s0_last[:] if (t, c) == (0, 1) else s_acc[t][:, cols]
+                nc.tensor.matmul_mx(
+                    out=acc, lhsT=c_codes[:, t, :].bitcast(FP8X4), lhsT_scale=c_bytes[:, t, :],
+                    rhs=z_codes[:].bitcast(FP8X4), rhs_scale=z_bytes[:], start=True, stop=True,
+                )
+                if t == 0:
+                    nc.scalar.activation(s[0][:, cols], acc, COPY, scale=0.0625)
+        for t in range(1, PACK):
+            nc.vector.tensor_scalar(s[t][:], s_acc[t][:], 0.0625, None, ALU.mult)
+
+        y_bf = sb.tile([P, S, PACK], BF16, name="y_bf", align_bytes=64)
+        out_rows = out_0.rearrange("(p t) j -> p t j", t=PACK)
+        y, ra = [], []
+
+        def fetch(t):
+            y_t = sb.tile([P, S], F32, name=f"y{t}")
+            nc.vector.tensor_copy(y_t[:], s[t][:])
+            old = sb.tile([P, W], F32, name=f"old{t}")
+            pa = sb.tile([P, W], F32, name=f"pa{t}")
+            nc.scalar.activation(old[:], s[t][:].indirect(n4_l[:]), COPY)
+            nc.scalar.activation(pa[:], s[t][:].indirect(n5_l[:]), COPY)
+            ra_t = sb.tile([P, W], F32, name=f"ra{t}")
+            nc.vector.scalar_tensor_tensor(ra_t[:], pa[:], -0.5, old[:], ALU.mult, ALU.add)
+            y.append(y_t)
+            ra.append(ra_t)
+
+        def put(t):
+            nc.scalar.activation(y[t][:].indirect(n4_l[:]), ra[t][:], COPY)
+            nc.vector.tensor_copy(y_bf[:, :, t], y[t][:])
+            queue = nc.scalar if t == PACK - 1 else nc.sync
+            queue.dma_start(out_rows[:, t, :], y[t][:])
+
+        fetch(0)
+        for t in range(1, PACK):
+            fetch(t)
+            put(t - 1)
+        put(PACK - 1)
+
+        y_codes = sb.tile([P, S], U32, name="y_codes", align_bytes=64)
+        y_bytes = sb.tile([P, S], U8, name="y_bytes", align_bytes=64)
+        nc.vector.quantize_mx(
+            out=y_codes[:].bitcast(FP8X4), scales=y_bytes[:], in_=y_bf[:].rearrange("p j t -> p (j t)")
+        )
+        nc.sync.dma_start(out_1[0].rearrange("p c r -> p (c r)").bitcast(I32), y_codes[:].bitcast(I32))
+        for q in range(4):
+            queue = nc.scalar if q % 2 == 0 else nc.sync
+            queue.dma_start(out_2[0, 4 * q : 4 * q + 4, :].bitcast(I32), y_bytes[32 * q : 32 * q + 4, :].bitcast(I32))

@@ -28,6 +28,7 @@ def tile_picked_pqhcgapmxkdif_none_po_kernel(
     with ExitStack() as ctx:
         lists = ctx.enter_context(tc.tile_pool(name="lists", bufs=1))
         sb = ctx.enter_context(tc.tile_pool(name="sb", bufs=1))
+        head = ctx.enter_context(tc.tile_pool(name="head", bufs=1))
         ps = ctx.enter_context(tc.psum_pool(name="ps", bufs=1))
 
         def load_list(name, src):
@@ -40,34 +41,36 @@ def tile_picked_pqhcgapmxkdif_none_po_kernel(
             nc.vector.memset(tile[:].bitcast(I32), 0)
             return tile
 
-        def load_scale_rows(tile, src):
-            nc.sync.dma_start(tile[0:P:8, :].bitcast(I32), src[0].bitcast(I32))
+        def load_scale_rows(queue, tile, src):
+            queue.dma_start(tile[0:P:8, :].bitcast(I32), src[0].bitcast(I32))
 
         def load_words(name, src, width):
-            tile = sb.tile([P, width], U32, name=name, align_bytes=64)
-            nc.scalar.dma_start(tile[:].bitcast(I32), src[0].rearrange("p c r -> p (c r)").bitcast(I32))
+            tile = sb.tile([P, width], U32, name=name, tag=name, align_bytes=64)
+            nc.sync.dma_start(tile[:].bitcast(I32), src[0].rearrange("p c r -> p (c r)").bitcast(I32))
             return tile
 
-        def place_scale_rows(queue, dst, src):
+        def place_scale_rows(queues, dst, src):
             for r in range(4):
+                queue = queues[r % len(queues)]
                 queue.dma_start(dst[r:P:32, :].bitcast(I32), src[8 * r : P : 32, :].bitcast(I32))
 
-        def deal(dst, src, t0, t1):
-            nc.vector.tensor_copy(dst[:, t0:t1, :], src.rearrange("p (m t) -> p t m", t=PACK)[:, t0:t1, :])
+        def deal(dst, src):
+            nc.vector.tensor_copy(dst.rearrange("p (t m) -> p m t", t=PACK), src.rearrange("p (m t) -> p m t", t=PACK))
 
-        d_scale_tab = zeroed_bytes("d_scale_tab", G)
+        d_scale_tab = head.tile([P, G], U8, name="d_scale_tab", offset=0, align_bytes=64)
+        nc.vector.memset(d_scale_tab[:].bitcast(I32), 0)
         x_scale_tab = sb.tile([P, T], U8, name="x_scale_tab", align_bytes=64)
         nc.gpsimd.memset(x_scale_tab[:].bitcast(I32), 0)
+        load_scale_rows(nc.scalar, d_scale_tab, d_scales)
+        load_scale_rows(nc.sync, x_scale_tab, x_scales)
         k1_l = load_list("k1_l", k1)
-        load_scale_rows(d_scale_tab, d_scales)
         offs_l = load_list("offs_l", offs)
-        load_scale_rows(x_scale_tab, x_scales)
-        d_tab = load_words("d_tab", d_words, G)
-        x_tab = load_words("x_tab", x_words, T)
         n1_l = load_list("n1_l", n1)
         n2_l = load_list("n2_l", n2)
-        n3_l = load_list("n3_l", n3)
+        d_tab = load_words("d_tab", d_words, G)
         cand_l = load_list("cand_l", cand)
+        n3_l = load_list("n3_l", n3)
+        x_tab = load_words("x_tab", x_words, T)
         n4_l = load_list("n4_l", n4)
         n5_l = load_list("n5_l", n5)
         gain = sb.tile([P, PACK], F32, name="gain")
@@ -75,99 +78,145 @@ def tile_picked_pqhcgapmxkdif_none_po_kernel(
         placed1 = zeroed_bytes("placed1", H + S)
         placed2 = zeroed_bytes("placed2", C)
 
-        picked1 = sb.tile([P, H + S], U8, name="picked1", align_bytes=64)
+        picked1 = sb.tile([P, H + S], U8, name="picked1", tag="bytes", align_bytes=64)
         nc.vector.tensor_copy(picked1[:, :H], d_scale_tab[:].indirect(k1_l[:]))
         nc.vector.tensor_copy(picked1[:, H:], x_scale_tab[:].indirect(offs_l[:]))
-        place_scale_rows(nc.scalar, placed1, picked1)
-        d_picked = sb.tile([P, H], U32, name="d_picked", align_bytes=64)
+        place_scale_rows([nc.sync], placed1, picked1)
+        d_picked = head.tile([P, H], U32, name="d_picked", offset=4 * S, align_bytes=64)
         nc.vector.tensor_copy(d_picked[:], d_tab[:].indirect(k1_l[:]))
-        d_codes = sb.tile([P, PACK, P], U32, name="d_codes", align_bytes=64)
-        d_bytes = sb.tile([P, PACK, P], U8, name="d_bytes", align_bytes=64)
-        deal(d_codes, d_picked[:], 0, 1)
-        xq = sb.tile([P, S], U32, name="xq", tag="xq", align_bytes=64)
+        d_codes = sb.tile([P, H], U32, name="d_codes", align_bytes=64)
+        deal(d_codes[:], d_picked[:])
+        xq = head.tile([P, S], U32, name="xq", offset=0, align_bytes=64)
         nc.vector.tensor_copy(xq[:], x_tab[:].indirect(offs_l[:]))
-        deal(d_bytes, placed1[:, :H], 0, 1)
-        deal(d_codes, d_picked[:], 1, PACK)
-        deal(d_bytes, placed1[:, :H], 1, PACK)
+        d_bytes = sb.tile([P, H], U8, name="d_bytes", align_bytes=64)
+        for t0, t1 in ((0, 1), (1, PACK)):
+            nc.vector.tensor_copy(
+                d_bytes[:].rearrange("p (t m) -> p m t", t=PACK)[:, :, t0:t1],
+                placed1[:, :H].rearrange("p (m t) -> p m t", t=PACK)[:, :, t0:t1],
+            )
+        dealt2 = sb.tile([P, C], U8, name="dealt2", align_bytes=64)
 
-        h = []
+        h_acc = []
         for t in range(PACK):
             acc = ps.tile([P, S], F32, name=f"h_acc{t}", tag=f"bank{t}")
             nc.tensor.matmul_mx(
-                out=acc[:], lhsT=d_codes[:, t, :].bitcast(FP8X4), lhsT_scale=d_bytes[:, t, :],
+                out=acc[:], lhsT=d_codes[:, t * P : (t + 1) * P].bitcast(FP8X4), lhsT_scale=d_bytes[:, t * P : (t + 1) * P],
                 rhs=xq[:].bitcast(FP8X4), rhs_scale=placed1[:, H:], start=True, stop=True,
             )
-            h_t = sb.tile([P, WIN], F32, name=f"h{t}", tag=f"h{t}", align_bytes=64)
+            h_acc.append(acc)
+
+        z_bf = sb.tile([P, S * PACK], BF16, name="z_bf", align_bytes=64)
+        z_slots = z_bf[:].rearrange("p (j t) -> p j t", t=PACK)
+        h, a, b, st, g, m = {}, {}, {}, {}, {}, {}
+
+        def leave_h(t, tag):
+            h[t] = sb.tile([P, WIN], F32, name=f"h{t}", tag=tag, align_bytes=64)
             if t == 0:
-                nc.scalar.activation(h_t[:, :S], acc[:], COPY, scale=0.0625)
+                nc.scalar.activation(h[t][:, :S], h_acc[t][:], COPY, scale=0.0625)
             else:
-                nc.vector.tensor_scalar(h_t[:, :S], acc[:], 0.0625, None, ALU.mult)
-            h.append(h_t)
+                nc.vector.tensor_scalar(h[t][:, :S], h_acc[t][:], 0.0625, None, ALU.mult)
 
-        z_bf = [sb.tile([P, HALF, PACK], BF16, name=f"z_bf{c}", align_bytes=64) for c in range(2)]
-        st = []
+        def fetch_a(t):
+            a[t] = sb.tile([P, S], F32, name=f"a{t}", tag=f"a{t}", align_bytes=64)
+            nc.scalar.activation(a[t][:], h[t][:].indirect(n1_l[:]), COPY)
 
-        def differences(t):
-            a = sb.tile([P, S], F32, name=f"a{t}")
-            b = sb.tile([P, S], F32, name=f"b{t}")
-            nc.scalar.activation(a[:], h[t][:].indirect(n1_l[:]), COPY)
-            nc.scalar.activation(b[:], h[t][:].indirect(n2_l[:]), COPY)
-            st_t = sb.tile([P, WIN], F32, name=f"st{t}")
-            nc.vector.tensor_tensor(st_t[:, :S], a[:], b[:], ALU.subtract)
-            st.append(st_t)
+        def fetch_b(t):
+            b[t] = sb.tile([P, S], F32, name=f"b{t}", tag=f"b{t}", align_bytes=64)
+            nc.scalar.activation(b[t][:], h[t][:].indirect(n2_l[:]), COPY)
 
-        def larger(t, c0, c1):
-            cols = slice(c0 * HALF, c1 * HALF)
-            width = (c1 - c0) * HALF
-            g = sb.tile([P, width], F32, name=f"g{t}_{c0}")
-            nc.scalar.activation(g[:], st[t][:].indirect(n3_l[:, c0 * HALF // 16 : c1 * HALF // 16]), COPY)
-            m = sb.tile([P, width], F32, name=f"m{t}_{c0}")
-            nc.vector.tensor_tensor(m[:], g[:], st[t][:, cols], ALU.max)
-            for c in range(c0, c1):
-                nc.vector.tensor_scalar(
-                    z_bf[c][:, :, t], m[:, (c - c0) * HALF : (c - c0 + 1) * HALF], gain[:, t : t + 1], None, ALU.mult
-                )
+        def subtract(t, tag):
+            st[t] = sb.tile([P, WIN], F32, name=f"st{t}", tag=tag, align_bytes=64)
+            nc.vector.tensor_tensor(st[t][:, :S], a[t][:], b[t][:], ALU.subtract)
 
-        differences(0)
-        differences(1)
-        picked2 = sb.tile([P, C], U8, name="picked2", tag="xq", align_bytes=64)
-        nc.vector.tensor_copy(picked2[:], x_scale_tab[:].indirect(cand_l[:]))
-        place_scale_rows(nc.sync, placed2, picked2)
-        larger(0, 0, 2)
-        differences(2)
-        c_picked = sb.tile([P, C], U32, name="c_picked", tag="h0", align_bytes=64)
+        def fetch_g(t, c0, c1):
+            g[t, c0] = sb.tile([P, (c1 - c0) * HALF], F32, name=f"g{t}_{c0}")
+            nc.scalar.activation(g[t, c0][:], st[t][:].indirect(n3_l[:, c0 * HALF // 16 : c1 * HALF // 16]), COPY)
+
+        def larger(t, c0, c1, tag=""):
+            m[t, c0] = sb.tile([P, (c1 - c0) * HALF], F32, name=f"m{t}_{c0}", tag=tag or f"m{t}_{c0}", align_bytes=64)
+            nc.vector.tensor_tensor(m[t, c0][:], g[t, c0][:], st[t][:, c0 * HALF : c1 * HALF], ALU.max)
+
+        def weigh(t, c0, c1):
+            nc.vector.tensor_scalar(z_slots[:, c0 * HALF : c1 * HALF, t], m[t, c0][:], gain[:, t : t + 1], None, ALU.mult)
+
+        def pick_cand_bytes(half, tile):
+            nc.vector.tensor_copy(tile[:], x_scale_tab[:].indirect(cand_l[:, half * 16 : (half + 1) * 16]))
+
+        def deal_cand_bytes(half, tile):
+            nc.vector.tensor_copy(
+                dealt2[:].rearrange("p (t m) -> p m t", t=PACK)[:, half * 64 : (half + 1) * 64, :],
+                tile[:].rearrange("p (m t) -> p m t", t=PACK),
+            )
+
+        leave_h(0, "h0")
+        fetch_a(0)
+        fetch_b(0)
+        picked2a = sb.tile([P, C // 2], U8, name="picked2a", tag="bytes", align_bytes=64)
+        pick_cand_bytes(0, picked2a)
+        leave_h(1, "h1")
+        fetch_a(1)
+        fetch_b(1)
+        leave_h(2, "h2")
+        fetch_a(2)
+        fetch_b(2)
+        picked2b = head.tile([P, C // 2], U8, name="picked2b", offset=0, align_bytes=64)
+        pick_cand_bytes(1, picked2b)
+        deal_cand_bytes(0, picked2a)
+        deal_cand_bytes(1, picked2b)
+        place_scale_rows([nc.sync], placed2, dealt2)
+        subtract(0, "st0")
+        fetch_g(0, 0, 2)
+        subtract(1, "st1")
+        fetch_g(1, 0, 2)
+        c_picked = sb.tile([P, C], U32, name="c_picked", tag="bytes", align_bytes=64)
         nc.vector.tensor_copy(c_picked[:], x_tab[:].indirect(cand_l[:]))
+        leave_h(3, "a1")
+        fetch_a(3)
+        fetch_b(3)
+        subtract(2, "b1")
+        fetch_g(2, 0, 2)
+        c_codes = sb.tile([P, C], U32, name="c_codes", align_bytes=64)
+        deal(c_codes[:], c_picked[:])
+        larger(0, 0, 2, "a2")
         larger(1, 0, 2)
-        c_codes = sb.tile([P, PACK, P], U32, name="c_codes", align_bytes=64)
-        c_bytes = sb.tile([P, PACK, P], U8, name="c_bytes", align_bytes=64)
-        deal(c_codes, c_picked[:], 0, PACK)
-        deal(c_bytes, placed2[:], 0, PACK)
-        differences(3)
+        weigh(0, 0, 2)
+        subtract(3, "st3")
+        fetch_g(3, 0, 1)
+        fetch_g(3, 1, 2)
+        weigh(1, 0, 2)
         larger(2, 0, 2)
+        larger(3, 0, 1)
+        weigh(2, 0, 2)
+        larger(3, 1, 2)
 
         s = [sb.tile([P, S], F32, name=f"s{t}") for t in range(PACK)]
-        s_acc = [ps.tile([P, S], F32, name=f"s_acc{t}", tag=f"bank{t + 4 if t < 3 else 0}") for t in range(PACK)]
-        s0_last = ps.tile([P, HALF], F32, name="s0_last", tag="bank7")
-        for c in range(2):
-            larger(3, c, c + 1)
-            z_codes = sb.tile([P, HALF], U32, name=f"z_codes{c}", align_bytes=64)
-            z_bytes = sb.tile([P, HALF], U8, name=f"z_bytes{c}", align_bytes=64)
-            nc.vector.quantize_mx(
-                out=z_codes[:].bitcast(FP8X4), scales=z_bytes[:], in_=z_bf[c][:].rearrange("p j t -> p (j t)")
+        z_codes = sb.tile([P, S], U32, name="z_codes", align_bytes=64)
+        z_bytes = sb.tile([P, S], U8, name="z_bytes", align_bytes=64)
+
+        def scores(acc, t, cols):
+            nc.tensor.matmul_mx(
+                out=acc, lhsT=c_codes[:, t * P : (t + 1) * P].bitcast(FP8X4), lhsT_scale=placed2[:, t * P : (t + 1) * P],
+                rhs=z_codes[:, cols].bitcast(FP8X4), rhs_scale=z_bytes[:, cols], start=True, stop=True,
             )
+
+        for c in range(2):
+            weigh(3, c, c + 1)
+        for c in range(2):
             cols = slice(c * HALF, (c + 1) * HALF)
-            for t in range(PACK):
-                acc = s0_last[:] if (t, c) == (0, 1) else s_acc[t][:, cols]
-                nc.tensor.matmul_mx(
-                    out=acc, lhsT=c_codes[:, t, :].bitcast(FP8X4), lhsT_scale=c_bytes[:, t, :],
-                    rhs=z_codes[:].bitcast(FP8X4), rhs_scale=z_bytes[:], start=True, stop=True,
-                )
-                if t == 0:
-                    nc.scalar.activation(s[0][:, cols], acc, COPY, scale=0.0625)
+            nc.vector.quantize_mx(
+                out=z_codes[:, cols].bitcast(FP8X4), scales=z_bytes[:, cols], in_=z_bf[:, c * HALF * PACK : (c + 1) * HALF * PACK]
+            )
+            acc = ps.tile([P, HALF], F32, name=f"s0_acc{c}", tag=f"bank{4 + c}")
+            scores(acc[:], 0, cols)
+            nc.scalar.activation(s[0][:, cols], acc[:], COPY, scale=0.0625)
+        s_acc = {t: ps.tile([P, S], F32, name=f"s_acc{t}", tag=f"bank{(5 + t) % 8}") for t in range(1, PACK)}
+        for t in range(1, PACK):
+            scores(s_acc[t][:], t, slice(0, S))
         for t in range(1, PACK):
             nc.vector.tensor_scalar(s[t][:], s_acc[t][:], 0.0625, None, ALU.mult)
 
-        y_bf = sb.tile([P, S, PACK], BF16, name="y_bf", align_bytes=64)
+        y_bf = sb.tile([P, S * PACK], BF16, name="y_bf", align_bytes=64)
+        y_slots = y_bf[:].rearrange("p (j t) -> p j t", t=PACK)
         out_rows = out_0.rearrange("(p t) j -> p t j", t=PACK)
         y, ra = [], []
 
@@ -185,7 +234,9 @@ def tile_picked_pqhcgapmxkdif_none_po_kernel(
 
         def put(t):
             nc.scalar.activation(y[t][:].indirect(n4_l[:]), ra[t][:], COPY)
-            nc.vector.tensor_copy(y_bf[:, :, t], y[t][:])
+            width = HALF if t == PACK - 1 else S
+            for j in range(0, S, width):
+                nc.vector.tensor_copy(y_slots[:, j : j + width, t], y[t][:, j : j + width])
             queue = nc.scalar if t == PACK - 1 else nc.sync
             queue.dma_start(out_rows[:, t, :], y[t][:])
 
@@ -197,9 +248,11 @@ def tile_picked_pqhcgapmxkdif_none_po_kernel(
 
         y_codes = sb.tile([P, S], U32, name="y_codes", align_bytes=64)
         y_bytes = sb.tile([P, S], U8, name="y_bytes", align_bytes=64)
-        nc.vector.quantize_mx(
-            out=y_codes[:].bitcast(FP8X4), scales=y_bytes[:], in_=y_bf[:].rearrange("p j t -> p (j t)")
-        )
+        for c in range(2):
+            cols = slice(c * HALF, (c + 1) * HALF)
+            nc.vector.quantize_mx(
+                out=y_codes[:, cols].bitcast(FP8X4), scales=y_bytes[:, cols], in_=y_bf[:, c * HALF * PACK : (c + 1) * HALF * PACK]
+            )
         nc.sync.dma_start(out_1[0].rearrange("p c r -> p (c r)").bitcast(I32), y_codes[:].bitcast(I32))
         for q in range(4):
             queue = nc.scalar if q % 2 == 0 else nc.sync

from contextlib import ExitStack

import concourse.mybir as mybir

K, T, S, G, H, C, W = 512, 1024, 256, 2048, 512, 512, 192
FLOPS = 2 * K * H * S + 2 * K * C * S

F32 = mybir.dt.float32
BF16 = mybir.dt.bfloat16
I32 = mybir.dt.int32
U32 = mybir.dt.uint32
U16 = mybir.dt.uint16
U8 = mybir.dt.uint8
FP8X4 = mybir.dt.float8_e4m3fn_x4
ALU = mybir.AluOpType
COPY = mybir.ActivationFunctionType.Copy

P = 128
PACK = 4
HALF = S // 2
WIN = 2 * S


def tile_picked_pqhcgapmxkdif_none_po_kernel(
    tc, x_words, x_scales, d_words, d_scales, gs, offs, k1, n1, n2, n3, cand, n4, n5, out_0, out_1, out_2
):
    nc = tc.nc
    with ExitStack() as ctx:
        lists = ctx.enter_context(tc.tile_pool(name="lists", bufs=1))
        sb = ctx.enter_context(tc.tile_pool(name="sb", bufs=1))
        head = ctx.enter_context(tc.tile_pool(name="head", bufs=1))
        ps = ctx.enter_context(tc.psum_pool(name="ps", bufs=1))

        def load_list(name, src):
            tile = lists.tile(list(src.shape), U16, name=name)
            nc.sync.dma_start(tile[:], src)
            return tile

        def zeroed_bytes(name, width, tag=""):
            tile = sb.tile([P, width], U8, name=name, align_bytes=64)
            nc.vector.memset(tile[:].bitcast(I32), 0)
            return tile

        def load_scale_rows(queue, tile, src):
            queue.dma_start(tile[0:P:8, :].bitcast(I32), src[0].bitcast(I32))

        def load_words(name, src, width):
            tile = sb.tile([P, width], U32, name=name, tag=name, align_bytes=64)
            nc.sync.dma_start(tile[:].bitcast(I32), src[0].rearrange("p c r -> p (c r)").bitcast(I32))
            return tile

        def place_scale_rows(queues, dst, src):
            for r in range(4):
                queue = queues[r % len(queues)]
                queue.dma_start(dst[r:P:32, :].bitcast(I32), src[8 * r : P : 32, :].bitcast(I32))

        def deal(dst, src):
            nc.vector.tensor_copy(dst.rearrange("p (t m) -> p m t", t=PACK), src.rearrange("p (m t) -> p m t", t=PACK))

        d_scale_tab = head.tile([P, G], U8, name="d_scale_tab", offset=0, align_bytes=64)
        nc.vector.memset(d_scale_tab[:].bitcast(I32), 0)
        x_scale_tab = sb.tile([P, T], U8, name="x_scale_tab", align_bytes=64)
        nc.gpsimd.memset(x_scale_tab[:].bitcast(I32), 0)
        load_scale_rows(nc.scalar, d_scale_tab, d_scales)
        load_scale_rows(nc.sync, x_scale_tab, x_scales)
        k1_l = load_list("k1_l", k1)
        offs_l = load_list("offs_l", offs)
        n1_l = load_list("n1_l", n1)
        n2_l = load_list("n2_l", n2)
        d_tab = load_words("d_tab", d_words, G)
        cand_l = load_list("cand_l", cand)
        n3_l = load_list("n3_l", n3)
        x_tab = load_words("x_tab", x_words, T)
        n4_l = load_list("n4_l", n4)
        n5_l = load_list("n5_l", n5)
        gain = sb.tile([P, PACK], F32, name="gain")
        nc.gpsimd.dma_start(gain[:], gs.rearrange("(p t) o -> p (t o)", t=PACK))
        placed1 = zeroed_bytes("placed1", H + S)
        placed2 = zeroed_bytes("placed2", C)

        picked1 = sb.tile([P, H + S], U8, name="picked1", tag="bytes", align_bytes=64)
        nc.vector.tensor_copy(picked1[:, :H], d_scale_tab[:].indirect(k1_l[:]))
        nc.vector.tensor_copy(picked1[:, H:], x_scale_tab[:].indirect(offs_l[:]))
        place_scale_rows([nc.sync], placed1, picked1)
        d_picked = head.tile([P, H], U32, name="d_picked", offset=4 * S, align_bytes=64)
        nc.vector.tensor_copy(d_picked[:], d_tab[:].indirect(k1_l[:]))
        d_codes = sb.tile([P, H], U32, name="d_codes", align_bytes=64)
        deal(d_codes[:], d_picked[:])
        xq = head.tile([P, S], U32, name="xq", offset=0, align_bytes=64)
        nc.vector.tensor_copy(xq[:], x_tab[:].indirect(offs_l[:]))
        d_bytes = sb.tile([P, H], U8, name="d_bytes", align_bytes=64)
        for t0, t1 in ((0, 1), (1, PACK)):
            nc.vector.tensor_copy(
                d_bytes[:].rearrange("p (t m) -> p m t", t=PACK)[:, :, t0:t1],
                placed1[:, :H].rearrange("p (m t) -> p m t", t=PACK)[:, :, t0:t1],
            )
        dealt2 = sb.tile([P, C], U8, name="dealt2", align_bytes=64)

        h_acc = []
        for t in range(PACK):
            acc = ps.tile([P, S], F32, name=f"h_acc{t}", tag=f"bank{t}")
            nc.tensor.matmul_mx(
                out=acc[:], lhsT=d_codes[:, t * P : (t + 1) * P].bitcast(FP8X4), lhsT_scale=d_bytes[:, t * P : (t + 1) * P],
                rhs=xq[:].bitcast(FP8X4), rhs_scale=placed1[:, H:], start=True, stop=True,
            )
            h_acc.append(acc)

        z_bf = sb.tile([P, S * PACK], BF16, name="z_bf", align_bytes=64)
        z_slots = z_bf[:].rearrange("p (j t) -> p j t", t=PACK)
        h, a, b, st, g, m = {}, {}, {}, {}, {}, {}

        def leave_h(t, tag):
            h[t] = sb.tile([P, WIN], F32, name=f"h{t}", tag=tag, align_bytes=64)
            if t == 0:
                nc.scalar.activation(h[t][:, :S], h_acc[t][:], COPY, scale=0.0625)
            else:
                nc.vector.tensor_scalar(h[t][:, :S], h_acc[t][:], 0.0625, None, ALU.mult)

        def fetch_a(t):
            a[t] = sb.tile([P, S], F32, name=f"a{t}", tag=f"a{t}", align_bytes=64)
            nc.scalar.activation(a[t][:], h[t][:].indirect(n1_l[:]), COPY)

        def fetch_b(t):
            b[t] = sb.tile([P, S], F32, name=f"b{t}", tag=f"b{t}", align_bytes=64)
            nc.scalar.activation(b[t][:], h[t][:].indirect(n2_l[:]), COPY)

        def subtract(t, tag):
            st[t] = sb.tile([P, WIN], F32, name=f"st{t}", tag=tag, align_bytes=64)
            nc.vector.tensor_tensor(st[t][:, :S], a[t][:], b[t][:], ALU.subtract)

        def fetch_g(t, c0, c1):
            g[t, c0] = sb.tile([P, (c1 - c0) * HALF], F32, name=f"g{t}_{c0}")
            nc.scalar.activation(g[t, c0][:], st[t][:].indirect(n3_l[:, c0 * HALF // 16 : c1 * HALF // 16]), COPY)

        def larger(t, c0, c1, tag=""):
            m[t, c0] = sb.tile([P, (c1 - c0) * HALF], F32, name=f"m{t}_{c0}", tag=tag or f"m{t}_{c0}", align_bytes=64)
            nc.vector.tensor_tensor(m[t, c0][:], g[t, c0][:], st[t][:, c0 * HALF : c1 * HALF], ALU.max)

        def weigh(t, c0, c1):
            nc.vector.tensor_scalar(z_slots[:, c0 * HALF : c1 * HALF, t], m[t, c0][:], gain[:, t : t + 1], None, ALU.mult)

        def pick_cand_bytes(half, tile):
            nc.vector.tensor_copy(tile[:], x_scale_tab[:].indirect(cand_l[:, half * 16 : (half + 1) * 16]))

        def deal_cand_bytes(half, tile):
            nc.vector.tensor_copy(
                dealt2[:].rearrange("p (t m) -> p m t", t=PACK)[:, half * 64 : (half + 1) * 64, :],
                tile[:].rearrange("p (m t) -> p m t", t=PACK),
            )

        leave_h(0, "h0")
        fetch_a(0)
        fetch_b(0)
        picked2a = sb.tile([P, C // 2], U8, name="picked2a", tag="bytes", align_bytes=64)
        pick_cand_bytes(0, picked2a)
        leave_h(1, "h1")
        fetch_a(1)
        fetch_b(1)
        leave_h(2, "h2")
        fetch_a(2)
        fetch_b(2)
        picked2b = head.tile([P, C // 2], U8, name="picked2b", offset=0, align_bytes=64)
        pick_cand_bytes(1, picked2b)
        deal_cand_bytes(0, picked2a)
        deal_cand_bytes(1, picked2b)
        place_scale_rows([nc.sync], placed2, dealt2)
        subtract(0, "st0")
        fetch_g(0, 0, 2)
        subtract(1, "st1")
        fetch_g(1, 0, 2)
        c_picked = sb.tile([P, C], U32, name="c_picked", tag="bytes", align_bytes=64)
        nc.vector.tensor_copy(c_picked[:], x_tab[:].indirect(cand_l[:]))
        leave_h(3, "a1")
        fetch_a(3)
        fetch_b(3)
        subtract(2, "b1")
        fetch_g(2, 0, 2)
        c_codes = sb.tile([P, C], U32, name="c_codes", align_bytes=64)
        deal(c_codes[:], c_picked[:])
        larger(0, 0, 2, "a2")
        larger(1, 0, 2)
        weigh(0, 0, 2)
        subtract(3, "st3")
        fetch_g(3, 0, 1)
        fetch_g(3, 1, 2)
        weigh(1, 0, 2)
        larger(2, 0, 2)
        larger(3, 0, 1)
        weigh(2, 0, 2)
        larger(3, 1, 2)

        s = [sb.tile([P, S], F32, name=f"s{t}") for t in range(PACK)]
        z_codes = sb.tile([P, S], U32, name="z_codes", align_bytes=64)
        z_bytes = sb.tile([P, S], U8, name="z_bytes", align_bytes=64)

        def scores(acc, t, cols):
            nc.tensor.matmul_mx(
                out=acc, lhsT=c_codes[:, t * P : (t + 1) * P].bitcast(FP8X4), lhsT_scale=placed2[:, t * P : (t + 1) * P],
                rhs=z_codes[:, cols].bitcast(FP8X4), rhs_scale=z_bytes[:, cols], start=True, stop=True,
            )

        for c in range(2):
            weigh(3, c, c + 1)
        for c in range(2):
            cols = slice(c * HALF, (c + 1) * HALF)
            nc.vector.quantize_mx(
                out=z_codes[:, cols].bitcast(FP8X4), scales=z_bytes[:, cols], in_=z_bf[:, c * HALF * PACK : (c + 1) * HALF * PACK]
            )
            acc = ps.tile([P, HALF], F32, name=f"s0_acc{c}", tag=f"bank{4 + c}")
            scores(acc[:], 0, cols)
            nc.scalar.activation(s[0][:, cols], acc[:], COPY, scale=0.0625)
        s_acc = {t: ps.tile([P, S], F32, name=f"s_acc{t}", tag=f"bank{(5 + t) % 8}") for t in range(1, PACK)}
        for t in range(1, PACK):
            scores(s_acc[t][:], t, slice(0, S))
        for t in range(1, PACK):
            nc.vector.tensor_scalar(s[t][:], s_acc[t][:], 0.0625, None, ALU.mult)

        y_bf = sb.tile([P, S * PACK], BF16, name="y_bf", align_bytes=64)
        y_slots = y_bf[:].rearrange("p (j t) -> p j t", t=PACK)
        out_rows = out_0.rearrange("(p t) j -> p t j", t=PACK)
        y, ra = [], []

        def fetch(t):
            y_t = sb.tile([P, S], F32, name=f"y{t}")
            nc.vector.tensor_copy(y_t[:], s[t][:])
            old = sb.tile([P, W], F32, name=f"old{t}")
            pa = sb.tile([P, W], F32, name=f"pa{t}")
            nc.scalar.activation(old[:], s[t][:].indirect(n4_l[:]), COPY)
            nc.scalar.activation(pa[:], s[t][:].indirect(n5_l[:]), COPY)
            ra_t = sb.tile([P, W], F32, name=f"ra{t}")
            nc.vector.scalar_tensor_tensor(ra_t[:], pa[:], -0.5, old[:], ALU.mult, ALU.add)
            y.append(y_t)
            ra.append(ra_t)

        def put(t):
            nc.scalar.activation(y[t][:].indirect(n4_l[:]), ra[t][:], COPY)
            width = HALF if t == PACK - 1 else S
            for j in range(0, S, width):
                nc.vector.tensor_copy(y_slots[:, j : j + width, t], y[t][:, j : j + width])
            queue = nc.scalar if t == PACK - 1 else nc.sync
            queue.dma_start(out_rows[:, t, :], y[t][:])

        fetch(0)
        for t in range(1, PACK):
            fetch(t)
            put(t - 1)
        put(PACK - 1)

        y_codes = sb.tile([P, S], U32, name="y_codes", align_bytes=64)
        y_bytes = sb.tile([P, S], U8, name="y_bytes", align_bytes=64)
        for c in range(2):
            cols = slice(c * HALF, (c + 1) * HALF)
            nc.vector.quantize_mx(
                out=y_codes[:, cols].bitcast(FP8X4), scales=y_bytes[:, cols], in_=y_bf[:, c * HALF * PACK : (c + 1) * HALF * PACK]
            )
        nc.sync.dma_start(out_1[0].rearrange("p c r -> p (c r)").bitcast(I32), y_codes[:].bitcast(I32))
        for q in range(4):
            queue = nc.scalar if q % 2 == 0 else nc.sync
            queue.dma_start(out_2[0, 4 * q : 4 * q + 4, :].bitcast(I32), y_bytes[32 * q : 32 * q + 4, :].bitcast(I32))
